import numpy as np, ml_dtypes
CORES = [0,1]
N = 2
def setup_inputs(rng):
    return {"x": rng.standard_normal((N, 128, 2048), dtype=np.float32).astype(ml_dtypes.bfloat16)}
def reference(x):
    g = np.concatenate(list(x), axis=1)
    return {"y": np.broadcast_to(g, (N,) + g.shape)}

W = 2048

SCRATCH = {
    "stage": ("sbuf", [128, W], "bfloat16"),
    "land": ("sbuf", [128, W], "bfloat16"),
}
SEMAPHORES = ["loaded", "arrived", "sent", "stored", "own"]


def rank_program(g, core, T, topo):
    rank = T.rank_of(core)
    if rank is None:
        return
    peer_rank = 1 - rank
    peer = T.cores[peer_rank]
    rid, pid, _se = topo.addr(peer)

    g.scalar.dma_start(T.y[:, rank * W:(rank + 1) * W], T.x[:]).then_inc(T.sem.own, 16)

    g.sync.dma_start(T.stage[:], T.x[:]).then_inc(T.sem.loaded, 16)

    g.wait_ge(T.sem.loaded, 16)
    g.remote_dma(T.land[:], T.stage[:], remote_sem=T.sem.arrived, local_sem=T.sem.sent,
                 pid=pid, routing_id=rid, dma_engine_mask=topo.mask(core, peer))

    g.sync.wait_ge(T.sem.arrived, 16)
    g.sync.dma_start(T.y[:, peer_rank * W:(peer_rank + 1) * W], T.land[:]).then_inc(T.sem.stored, 16)

    g.wait_ge(T.sem.sent, 16)
    g.wait_ge(T.sem.own, 16)
    g.wait_ge(T.sem.stored, 16)
